import numpy as np
import ml_dtypes

BF16 = ml_dtypes.bfloat16


def bf(x):
    return np.asarray(x, np.float32).astype(BF16)


def f32(x):
    return np.asarray(x, np.float32)


def f64(x):
    return np.asarray(x).astype(np.float64)


def striped(idx):
    return np.tile(idx.reshape(-1, 16).T, (8, 1))


S, K, M, N, V, D = 1024, 128, 256, 2048, 128, 16


def setup_inputs():
    return {"table": bf(np.random.standard_normal((K, S))), "w": bf(np.random.standard_normal((K, M)) / np.sqrt(K)), "c": f32((0.2 + 0.8 * np.random.random_sample((1, N))) / np.sqrt(D)), "offs": striped(np.random.permutation(np.tile(np.arange(S), 2))[:N])}


def reference(table, w, c, offs):
    idx = offs[:16].T.reshape(-1)
    y = (f64(w).T @ f64(table)[:, idx]).reshape(M, V, D)
    a = f64(c).reshape(V, D)
    z = (y * a).sum(axis=2)
    return z

@@ -1,0 +1,48 @@
+import concourse.mybir as mybir
+
+BF16, F32, U16 = mybir.dt.bfloat16, mybir.dt.float32, mybir.dt.uint16
+
+P = 128
+WORDS = 1024
+M = 256
+N = 2048
+BAG = 16
+PIECE = 512
+BLOCKS, PIECES, BAGS = M // P, N // PIECE, N // BAG
+PIECE_BAGS = PIECE // BAG
+
+FLOPS = 2 * P * M * N + 2 * M * N
+
+
+def tile_rows_wbag_none_rep_kernel(tc, table, w, c, offs, out):
+    nc = tc.nc
+    with (
+        tc.tile_pool(name="held", bufs=1) as held,
+        tc.psum_pool(name="psum", bufs=1) as psum,
+    ):
+        offsets = held.tile([P, N // BAG], U16, name="offsets")
+        window = held.tile([P, WORDS], BF16, name="window")
+        weights = held.tile([P, M], BF16, name="weights")
+        nc.sync.dma_start(window[:], table)
+        nc.sync.dma_start(offsets[:], offs)
+        nc.scalar.dma_start(weights[:], w)
+
+        factors = []
+        for piece in range(PIECES):
+            spread = held.tile([P, PIECE], F32, name=f"factors{piece}")
+            nc.sync.dma_start(spread[:], c[0, piece * PIECE:(piece + 1) * PIECE].partition_broadcast(P))
+            factors.append(spread)
+
+        sums = held.tile([P, BLOCKS, BAGS], F32, name="sums")
+        for piece in range(PIECES):
+            bags = slice(piece * PIECE_BAGS, (piece + 1) * PIECE_BAGS)
+            for block in range(BLOCKS):
+                y = psum.tile([P, PIECE], F32, name=f"y{piece}_{block}")
+                nc.tensor.matmul(y[:], weights[:, block * P:(block + 1) * P],
+                                 window[:].indirect(offsets[:, bags]), start=True, stop=True)
+                weighted = held.tile([P, PIECE], F32, name=f"weighted{piece}_{block}")
+                nc.vector.tensor_tensor(weighted[:], y[:], factors[piece][:], mybir.AluOpType.mult)
+                nc.vector.tensor_reduce(sums[:, block, bags],
+                                        weighted[:].rearrange("p (v t) -> p v t", t=BAG),
+                                        mybir.AxisListType.X, mybir.AluOpType.add)
+        nc.sync.dma_start(out.rearrange("(b p) v -> p b v", p=P), sums[:])

@@ -1,6 +1,7 @@
 import concourse.mybir as mybir
 
 BF16, F32, U16 = mybir.dt.bfloat16, mybir.dt.float32, mybir.dt.uint16
+MULT, ADD = mybir.AluOpType.mult, mybir.AluOpType.add
 
 P = 128
 WORDS = 1024
@@ -10,6 +11,7 @@ BAG = 16
 PIECE = 512
 BLOCKS, PIECES, BAGS = M // P, N // PIECE, N // BAG
 PIECE_BAGS = PIECE // BAG
+HALF = BAG // 2
 
 FLOPS = 2 * P * M * N + 2 * M * N
 
@@ -36,13 +38,20 @@ def tile_rows_wbag_none_rep_kernel(tc, table, w, c, offs, out):
         sums = held.tile([P, BLOCKS, BAGS], F32, name="sums")
         for piece in range(PIECES):
             bags = slice(piece * PIECE_BAGS, (piece + 1) * PIECE_BAGS)
+            weighted = held.tile([P, BLOCKS * PIECE_BAGS, BAG], F32, name=f"weighted{piece}")
             for block in range(BLOCKS):
-                y = psum.tile([P, PIECE], F32, name=f"y{piece}_{block}")
-                nc.tensor.matmul(y[:], weights[:, block * P:(block + 1) * P],
+                y = psum.tile([P, PIECE_BAGS, BAG], F32, name=f"y{piece}_{block}")
+                nc.tensor.matmul(y[:].rearrange("p v t -> p (v t)"), weights[:, block * P:(block + 1) * P],
                                  window[:].indirect(offsets[:, bags]), start=True, stop=True)
-                weighted = held.tile([P, PIECE], F32, name=f"weighted{piece}_{block}")
-                nc.vector.tensor_tensor(weighted[:], y[:], factors[piece][:], mybir.AluOpType.mult)
-                nc.vector.tensor_reduce(sums[:, block, bags],
-                                        weighted[:].rearrange("p (v t) -> p v t", t=BAG),
-                                        mybir.AxisListType.X, mybir.AluOpType.add)
+                nc.vector.tensor_tensor(weighted[:, block * PIECE_BAGS:(block + 1) * PIECE_BAGS, :], y[:],
+                                        factors[piece][:].rearrange("p (v t) -> p v t", t=BAG), MULT)
+            folded_blocks = BLOCKS if piece < PIECES - 1 else BLOCKS - 1
+            split = folded_blocks * PIECE_BAGS
+            folded = held.tile([P, split, HALF], F32, name=f"folded{piece}")
+            nc.gpsimd.tensor_tensor(folded[:], weighted[:, :split, :HALF], weighted[:, :split, HALF:], ADD)
+            for block in range(folded_blocks, BLOCKS):
+                nc.vector.tensor_reduce(sums[:, block, bags], weighted[:, split:, :], mybir.AxisListType.X, ADD)
+            nc.vector.tensor_reduce(sums[:, :folded_blocks, bags],
+                                    folded[:].rearrange("p (b v) t -> p b v t", v=PIECE_BAGS),
+                                    mybir.AxisListType.X, ADD)
         nc.sync.dma_start(out.rearrange("(b p) v -> p b v", p=P), sums[:])

@@ -1,4 +1,5 @@
 import concourse.mybir as mybir
+from concourse.masks import make_identity
 
 BF16, F32, U16 = mybir.dt.bfloat16, mybir.dt.float32, mybir.dt.uint16
 MULT, ADD = mybir.AluOpType.mult, mybir.AluOpType.add
@@ -12,6 +13,10 @@ PIECE = 512
 BLOCKS, PIECES, BAGS = M // P, N // PIECE, N // BAG
 PIECE_BAGS = PIECE // BAG
 HALF = BAG // 2
+QUAD = PIECE // P
+BANK = 2048
+RING = 4
+EARLY = 3
 
 FLOPS = 2 * P * M * N + 2 * M * N
 
@@ -28,23 +33,38 @@ def tile_rows_wbag_none_rep_kernel(tc, table, w, c, offs, out):
         nc.sync.dma_start(window[:], table)
         nc.sync.dma_start(offsets[:], offs)
         nc.scalar.dma_start(weights[:], w)
+        quads = held.tile([P, PIECES, 2 * QUAD], F32, name="quads")
+        nc.scalar.dma_start(quads[:, :, :QUAD], c.rearrange("o (q k r) -> (o k) q r", k=P, r=QUAD))
+        identity = held.tile([P, P], F32, name="identity")
+        make_identity(nc, identity[:])
 
-        factors = []
-        for piece in range(PIECES):
-            spread = held.tile([P, PIECE], F32, name=f"factors{piece}")
-            nc.sync.dma_start(spread[:], c[0, piece * PIECE:(piece + 1) * PIECE].partition_broadcast(P))
-            factors.append(spread)
+        turns = [0]
 
+        def next_bank(shape, name):
+            turns.append(turns[-1] + 1)
+            return psum.tile(shape, F32, name=name, offset=turns[-2] % RING * BANK)
+
+        def spread_factors(piece):
+            spread = next_bank([P, QUAD, P], f"spread{piece}")
+            for r in range(QUAD):
+                nc.tensor.transpose(spread[:, r, :], quads[:, piece, r:r + 1].to_broadcast([P, P]), identity[:])
+            factors = held.tile([P, PIECE_BAGS, BAG], F32, name=f"factors{piece}")
+            nc.scalar.copy(factors[:].rearrange("p v (k r) -> p (v k) r", r=QUAD),
+                           spread[:].rearrange("p r k -> p k r"))
+            return factors
+
+        early = [spread_factors(piece) for piece in range(EARLY)]
         sums = held.tile([P, BLOCKS, BAGS], F32, name="sums")
         for piece in range(PIECES):
             bags = slice(piece * PIECE_BAGS, (piece + 1) * PIECE_BAGS)
+            factors = early[piece] if piece < EARLY else spread_factors(piece)
             weighted = held.tile([P, BLOCKS * PIECE_BAGS, BAG], F32, name=f"weighted{piece}")
             for block in range(BLOCKS):
-                y = psum.tile([P, PIECE_BAGS, BAG], F32, name=f"y{piece}_{block}")
+                y = next_bank([P, PIECE_BAGS, BAG], f"y{piece}_{block}")
                 nc.tensor.matmul(y[:].rearrange("p v t -> p (v t)"), weights[:, block * P:(block + 1) * P],
                                  window[:].indirect(offsets[:, bags]), start=True, stop=True)
                 nc.vector.tensor_tensor(weighted[:, block * PIECE_BAGS:(block + 1) * PIECE_BAGS, :], y[:],
-                                        factors[piece][:].rearrange("p (v t) -> p v t", t=BAG), MULT)
+                                        factors[:], MULT)
             folded_blocks = BLOCKS if piece < PIECES - 1 else BLOCKS - 1
             split = folded_blocks * PIECE_BAGS
             folded = held.tile([P, split, HALF], F32, name=f"folded{piece}")

@@ -15,8 +15,7 @@ PIECE_BAGS = PIECE // BAG
 HALF = BAG // 2
 QUAD = PIECE // P
 BANK = 2048
-RING = 4
-EARLY = 3
+RING = PIECES + 1
 
 FLOPS = 2 * P * M * N + 2 * M * N
 
@@ -27,7 +26,7 @@ def tile_rows_wbag_none_rep_kernel(tc, table, w, c, offs, out):
         tc.tile_pool(name="held", bufs=1) as held,
         tc.psum_pool(name="psum", bufs=1) as psum,
     ):
-        offsets = held.tile([P, N // BAG], U16, name="offsets")
+        offsets = held.tile([P, BAGS], U16, name="offsets")
         window = held.tile([P, WORDS], BF16, name="window")
         weights = held.tile([P, M], BF16, name="weights")
         nc.sync.dma_start(window[:], table)
@@ -38,40 +37,37 @@ def tile_rows_wbag_none_rep_kernel(tc, table, w, c, offs, out):
         identity = held.tile([P, P], F32, name="identity")
         make_identity(nc, identity[:])
 
-        turns = [0]
-
-        def next_bank(shape, name):
-            turns.append(turns[-1] + 1)
-            return psum.tile(shape, F32, name=name, offset=turns[-2] % RING * BANK)
-
-        def spread_factors(piece):
-            spread = next_bank([P, QUAD, P], f"spread{piece}")
+        factors = []
+        for piece in range(PIECES):
+            spread = psum.tile([P, QUAD, P], F32, name=f"spread{piece}", offset=piece * BANK)
             for r in range(QUAD):
                 nc.tensor.transpose(spread[:, r, :], quads[:, piece, r:r + 1].to_broadcast([P, P]), identity[:])
-            factors = held.tile([P, PIECE_BAGS, BAG], F32, name=f"factors{piece}")
-            nc.scalar.copy(factors[:].rearrange("p v (k r) -> p (v k) r", r=QUAD),
+            in_order = held.tile([P, PIECE_BAGS, BAG], F32, name=f"factors{piece}")
+            nc.scalar.copy(in_order[:].rearrange("p v (k r) -> p (v k) r", r=QUAD),
                            spread[:].rearrange("p r k -> p k r"))
-            return factors
+            factors.append(in_order)
 
-        early = [spread_factors(piece) for piece in range(EARLY)]
+        def add_up(total, terms):
+            nc.vector.tensor_reduce(total, terms, mybir.AxisListType.X, ADD)
+
         sums = held.tile([P, BLOCKS, BAGS], F32, name="sums")
+        waiting = []
         for piece in range(PIECES):
             bags = slice(piece * PIECE_BAGS, (piece + 1) * PIECE_BAGS)
-            factors = early[piece] if piece < EARLY else spread_factors(piece)
-            weighted = held.tile([P, BLOCKS * PIECE_BAGS, BAG], F32, name=f"weighted{piece}")
+            fold = BLOCKS if piece < PIECES - 1 else BLOCKS - 1
+            folded = held.tile([P, fold, PIECE_BAGS, HALF], F32, name=f"folded{piece}")
             for block in range(BLOCKS):
-                y = next_bank([P, PIECE_BAGS, BAG], f"y{piece}_{block}")
+                bank = (PIECES + piece * BLOCKS + block) % RING
+                y = psum.tile([P, PIECE_BAGS, BAG], F32, name=f"y{piece}_{block}", offset=bank * BANK)
                 nc.tensor.matmul(y[:].rearrange("p v t -> p (v t)"), weights[:, block * P:(block + 1) * P],
                                  window[:].indirect(offsets[:, bags]), start=True, stop=True)
-                nc.vector.tensor_tensor(weighted[:, block * PIECE_BAGS:(block + 1) * PIECE_BAGS, :], y[:],
-                                        factors[:], MULT)
-            folded_blocks = BLOCKS if piece < PIECES - 1 else BLOCKS - 1
-            split = folded_blocks * PIECE_BAGS
-            folded = held.tile([P, split, HALF], F32, name=f"folded{piece}")
-            nc.gpsimd.tensor_tensor(folded[:], weighted[:, :split, :HALF], weighted[:, :split, HALF:], ADD)
-            for block in range(folded_blocks, BLOCKS):
-                nc.vector.tensor_reduce(sums[:, block, bags], weighted[:, split:, :], mybir.AxisListType.X, ADD)
-            nc.vector.tensor_reduce(sums[:, :folded_blocks, bags],
-                                    folded[:].rearrange("p (b v) t -> p b v t", v=PIECE_BAGS),
-                                    mybir.AxisListType.X, ADD)
+                weighted = held.tile([P, PIECE_BAGS, BAG], F32, name=f"weighted{piece}_{block}")
+                nc.vector.tensor_tensor(weighted[:], y[:], factors[piece][:], MULT)
+                if block < fold:
+                    nc.gpsimd.tensor_tensor(folded[:, block, :, :], weighted[:, :, :HALF], weighted[:, :, HALF:], ADD)
+            for total, terms in waiting:
+                add_up(total, terms)
+            waiting = [(sums[:, :fold, bags], folded[:])]
+        add_up(sums[:, BLOCKS - 1, bags], weighted[:])
+        add_up(*waiting[0])
         nc.sync.dma_start(out.rearrange("(b p) v -> p b v", p=P), sums[:])

import concourse.mybir as mybir
from concourse.masks import make_identity

BF16, F32, U16 = mybir.dt.bfloat16, mybir.dt.float32, mybir.dt.uint16
MULT, ADD = mybir.AluOpType.mult, mybir.AluOpType.add

P = 128
WORDS = 1024
M = 256
N = 2048
BAG = 16
PIECE = 512
BLOCKS, PIECES, BAGS = M // P, N // PIECE, N // BAG
PIECE_BAGS = PIECE // BAG
HALF = BAG // 2
QUAD = PIECE // P
BANK = 2048
RING = PIECES + 1

FLOPS = 2 * P * M * N + 2 * M * N


def tile_rows_wbag_none_rep_kernel(tc, table, w, c, offs, out):
    nc = tc.nc
    with (
        tc.tile_pool(name="held", bufs=1) as held,
        tc.psum_pool(name="psum", bufs=1) as psum,
    ):
        offsets = held.tile([P, BAGS], U16, name="offsets")
        window = held.tile([P, WORDS], BF16, name="window")
        weights = held.tile([P, M], BF16, name="weights")
        nc.sync.dma_start(window[:], table)
        nc.sync.dma_start(offsets[:], offs)
        nc.scalar.dma_start(weights[:], w)
        quads = held.tile([P, PIECES, 2 * QUAD], F32, name="quads")
        nc.scalar.dma_start(quads[:, :, :QUAD], c.rearrange("o (q k r) -> (o k) q r", k=P, r=QUAD))
        identity = held.tile([P, P], F32, name="identity")
        make_identity(nc, identity[:])

        factors = []
        for piece in range(PIECES):
            spread = psum.tile([P, QUAD, P], F32, name=f"spread{piece}", offset=piece * BANK)
            for r in range(QUAD):
                nc.tensor.transpose(spread[:, r, :], quads[:, piece, r:r + 1].to_broadcast([P, P]), identity[:])
            in_order = held.tile([P, PIECE_BAGS, BAG], F32, name=f"factors{piece}")
            nc.scalar.copy(in_order[:].rearrange("p v (k r) -> p (v k) r", r=QUAD),
                           spread[:].rearrange("p r k -> p k r"))
            factors.append(in_order)

        def add_up(total, terms):
            nc.vector.tensor_reduce(total, terms, mybir.AxisListType.X, ADD)

        sums = held.tile([P, BLOCKS, BAGS], F32, name="sums")
        waiting = []
        for piece in range(PIECES):
            bags = slice(piece * PIECE_BAGS, (piece + 1) * PIECE_BAGS)
            fold = BLOCKS if piece < PIECES - 1 else BLOCKS - 1
            folded = held.tile([P, fold, PIECE_BAGS, HALF], F32, name=f"folded{piece}")
            for block in range(BLOCKS):
                bank = (PIECES + piece * BLOCKS + block) % RING
                y = psum.tile([P, PIECE_BAGS, BAG], F32, name=f"y{piece}_{block}", offset=bank * BANK)
                nc.tensor.matmul(y[:].rearrange("p v t -> p (v t)"), weights[:, block * P:(block + 1) * P],
                                 window[:].indirect(offsets[:, bags]), start=True, stop=True)
                weighted = held.tile([P, PIECE_BAGS, BAG], F32, name=f"weighted{piece}_{block}")
                nc.vector.tensor_tensor(weighted[:], y[:], factors[piece][:], MULT)
                if block < fold:
                    nc.gpsimd.tensor_tensor(folded[:, block, :, :], weighted[:, :, :HALF], weighted[:, :, HALF:], ADD)
            for total, terms in waiting:
                add_up(total, terms)
            waiting = [(sums[:, :fold, bags], folded[:])]
        add_up(sums[:, BLOCKS - 1, bags], weighted[:])
        add_up(*waiting[0])
        nc.sync.dma_start(out.rearrange("(b p) v -> p b v", p=P), sums[:])
